import numpy as np
import ml_dtypes


def mxq(x, axis, fmt="e4m3"):
    dtype, down = {"e4m3": (ml_dtypes.float8_e4m3fn, 7), "e5m2": (ml_dtypes.float8_e5m2, 14)}[fmt]
    v = np.moveaxis(np.asarray(x, np.float32).astype(ml_dtypes.bfloat16).astype(np.float64), axis, -1)
    blocks = v.reshape(v.shape[:-1] + (-1, 32))
    amax = np.abs(blocks).max(-1, keepdims=True)
    byte = np.maximum(np.where(amax > 0, np.frexp(amax)[1] - 1 + 127, 0) - down, 1)
    scale = np.exp2(byte - 127.0)
    codes = (blocks / scale).astype(np.float32).astype(dtype).astype(np.float64)
    return np.moveaxis((codes * scale).reshape(v.shape), -1, axis)


WIDE = False


def mx_kscale(k):
    if not WIDE:
        return np.ones(k)
    levels = np.array([10, -10, 5, -5, 0])
    if k % 512:
        return np.exp2(np.random.permutation(np.resize(levels, k // 32))).repeat(32)
    a = np.empty((k // 512, 16))
    for p in range(k // 512):
        a[p, :8] = np.random.permutation(np.resize(levels, 8))
        for g in range(8):
            far = levels[np.abs(levels - a[p, g]) >= 10]
            a[p, g + 8] = far[np.random.randint(len(far))]
    return np.exp2(a.ravel()).repeat(32)


def f64(x):
    return np.asarray(x).astype(np.float64)


def striped(idx):
    return np.tile(idx.reshape(-1, 16).T, (8, 1)).astype(np.uint16)


def unstriped(offs):
    return offs[:16].T.reshape(-1).astype(np.int64)


def pack_weight(w):
    k, n = w.shape
    w = f64(np.asarray(w, np.float32).astype(ml_dtypes.bfloat16)).reshape(k // 32, 32, n)
    amax = np.abs(w).max(1)
    byte = np.clip(np.where(amax > 0, np.frexp(amax)[1] - 1 + 127 - 7, 1), 1, 254)
    scaled = (w * np.exp2(127.0 - byte)[:, None, :]).reshape(k, n).astype(np.float32)
    words = np.ascontiguousarray(scaled.reshape(k // 512, 128, 4, n).transpose(0, 1, 3, 2)).astype(ml_dtypes.float8_e4m3fn).view(np.uint8)
    return words, np.ascontiguousarray(byte.astype(np.uint8).reshape(k // 512, 16, n))


def unpack_weight(words, scales):
    g, p, n, _ = words.shape
    vals = np.ascontiguousarray(words).view(ml_dtypes.float8_e4m3fn).astype(np.float64) * np.repeat(np.exp2(scales.astype(np.float64) - 127.0), 8, axis=1)[..., None]
    return vals.transpose(0, 1, 3, 2).reshape(g * 512, n)


def silu(v):
    return v / (1.0 + np.exp(-np.maximum(v, -700.0)))


K, T, E, C, N = 1536, 512, 4, 256, 256


def by_expert(wq, xq):
    return np.concatenate([wq[e].T @ xq[:, e * C:(e + 1) * C] for e in range(E)], axis=1)


def setup_inputs():
    n = np.random.standard_normal
    s = mx_kscale(K)[:, None]
    first = np.random.permutation(np.repeat(np.arange(E), T // E))
    second = (first + 1 + np.random.permutation(np.repeat(np.arange(E - 1), -(-T // (E - 1)))[:T])) % E
    while np.bincount(second, minlength=E).max() != T // E:
        load = np.bincount(second, minlength=E); hi, lo = int(load.argmax()), int(load.argmin())
        t = np.flatnonzero((second == hi) & (first != lo))[0]; second[t] = lo
    slot_token = np.empty(E * C, np.int64); pos = np.empty((2, T), np.int64); fill = np.zeros(E, np.int64)
    place = np.stack([np.random.permutation(C) for _ in range(E)])
    for r, deal in enumerate((first, second)):
        for t in np.random.permutation(T):
            e = deal[t]; j = e * C + place[e, fill[e]]; fill[e] += 1; slot_token[j] = t; pos[r, t] = j
    g = np.random.uniform(0.2, 0.8, T)
    packed = [pack_weight(m) for m in n((E, K, N)) / np.sqrt(K) / s[None]]
    return {
        "xT": (n((K, T)) * s).astype(np.float32),
        "w_words": np.stack([m[0] for m in packed]),
        "w_scales": np.stack([m[1] for m in packed]),
        "b": (0.3 * n((N, E))).astype(np.float32),
        "gate": np.stack([np.tile(g, (N, 1)), np.tile(1.0 - g, (N, 1))]).astype(np.float32),
        "offs": striped(slot_token),
        "pos1": striped(pos[0]),
        "pos2": striped(pos[1]),
    }


def reference(xT, w_words, w_scales, b, gate, offs, pos1, pos2):
    idx = unstriped(offs)
    xq = mxq(f64(xT)[:, idx], 0, "e4m3")
    w = np.stack([unpack_weight(w_words[e], w_scales[e]) for e in range(E)])
    y = by_expert(w, xq)
    y = silu(y + np.repeat(f64(b), C, axis=1))
    return f64(gate[0]) * y[:, unstriped(pos1)] + f64(gate[1]) * y[:, unstriped(pos2)]

@@ -1,0 +1,166 @@
+from contextlib import ExitStack
+
+import concourse.mybir as mybir
+
+K, T, E, C, N = 1536, 512, 4, 256, 256
+P = 128
+PACK = 4
+PASSES = K // (P * PACK)
+BLOCKS = N // P
+SLOTS = E * C
+HALF = T // 2
+FLOPS = 2 * SLOTS * K * N
+
+F32 = mybir.dt.float32
+BF16 = mybir.dt.bfloat16
+U32 = mybir.dt.uint32
+I32 = mybir.dt.int32
+U16 = mybir.dt.uint16
+U8 = mybir.dt.uint8
+FP8X4 = mybir.dt.float8_e4m3fn_x4
+SILU = mybir.ActivationFunctionType.Silu
+MULT = mybir.AluOpType.mult
+ADD = mybir.AluOpType.add
+
+LOADS = (((0, 256), (256, 512)), ((0, 256), (256, 512)), ((0, 512),))
+CUTS = ((0, 384), (384, 768), (768, 1024))
+
+
+def tile_routed_moe_kernel(tc, xT, w_words, w_scales, b, gate, offs, pos1, pos2, out):
+    nc = tc.nc
+    with ExitStack() as ctx:
+        lists = ctx.enter_context(tc.tile_pool(name="lists", bufs=1))
+        keep = ctx.enter_context(tc.tile_pool(name="keep", bufs=1))
+        psum = ctx.enter_context(tc.psum_pool(name="psum", bufs=1))
+
+        offs_t = lists.tile([P, SLOTS // 16], U16, name="offs_t")
+        pos_t = [lists.tile([P, T // 16], U16, name="pos%d_t" % r) for r in range(2)]
+
+        warm = keep.tile([P, 1], F32, name="warm")
+        nc.gpsimd.memset(warm[:], 0.0)
+        warm_out = keep.tile([P, 1], F32, name="warm_out")
+        nc.scalar.activation(warm_out[:], warm[:], SILU)
+
+        token_scales = keep.tile([P, T], U8, name="token_scales", align_bytes=64)
+        nc.gpsimd.memset(token_scales[:], 0)
+        w_scale_t = keep.tile([P, E * PASSES * N], U8, name="w_scale_t", align_bytes=64)
+        nc.vector.memset(w_scale_t[:].bitcast(I32), 0)
+
+        raw = {}
+        for a in range(PASSES):
+            rows = xT[a * P * PACK : (a + 1) * P * PACK, :].rearrange("(p t) n -> p t n", t=PACK)
+            for lo, hi in LOADS[a]:
+                raw[a, lo] = keep.tile([P, PACK, hi - lo], F32, name="raw%d_%d" % (a, lo))
+                nc.sync.dma_start(out=raw[a, lo][:], in_=rows[:, :, lo:hi])
+                if a == 0 and lo == 0:
+                    nc.sync.dma_start(offs_t[:], offs)
+        bias_t = keep.tile([P, BLOCKS, E], F32, name="bias_t")
+        nc.scalar.dma_start(out=bias_t[:], in_=b.rearrange("(c p) e -> p c e", p=P))
+        sview = w_scales.rearrange("e a q n -> q (e a) n")
+        for q in range(4):
+            nc.sync.dma_start(
+                out=w_scale_t[32 * q : 32 * q + 4, :].rearrange("p (g n) -> p g n", n=N).bitcast(I32),
+                in_=sview[4 * q : 4 * q + 4].bitcast(I32),
+            )
+        w_t = {}
+        for e in range(E):
+            w_t[e] = keep.tile([P, PASSES, N], U32, name="w%d" % e, align_bytes=64)
+            nc.sync.dma_start(
+                out=w_t[e][:].bitcast(I32),
+                in_=w_words[e].rearrange("a p n r -> p a (n r)").bitcast(I32),
+            )
+        nc.sync.dma_start(pos_t[0][:], pos1)
+        nc.sync.dma_start(pos_t[1][:], pos2)
+        gate_t = {}
+        for c in range(BLOCKS):
+            for r in range(2):
+                gate_t[c, r] = keep.tile([P, T], F32, name="gate%d%d" % (c, r))
+                nc.sync.dma_start(out=gate_t[c, r][:], in_=gate[r, c * P : (c + 1) * P, :])
+
+        grouped = [keep.tile([P, T, PACK], BF16, name="grouped%d" % a, align_bytes=64) for a in range(PASSES)]
+        token_words = [keep.tile([P, T], U32, name="token_words%d" % a, align_bytes=64) for a in range(PASSES)]
+        slot_words = [keep.tile([P, SLOTS], U32, name="slot_words%d" % a, align_bytes=64) for a in range(PASSES)]
+        slot_scales = keep.tile([P, SLOTS], U8, name="slot_scales", align_bytes=64)
+
+        def interleave(a, load, lo, hi, copy):
+            copy(grouped[a][:, lo:hi, :], raw[a, load][:, :, lo - load : hi - load].rearrange("p t n -> p n t"))
+
+        def quantize(a, lo, hi):
+            nc.vector.quantize_mx(
+                out=token_words[a][:, lo:hi].bitcast(FP8X4),
+                scales=token_scales[4 * a : P, lo:hi],
+                in_=grouped[a][:, lo:hi, :].rearrange("p n t -> p (n t)"),
+            )
+
+        def gather_words(a, cut):
+            lo, hi = cut
+            nc.vector.tensor_copy(slot_words[a][:, lo:hi], token_words[a][:].indirect(offs_t[:, lo // 16 : hi // 16]))
+
+        def gather_scales(cut):
+            lo, hi = cut
+            nc.vector.tensor_copy(slot_scales[:, lo:hi], token_scales[:].indirect(offs_t[:, lo // 16 : hi // 16]))
+
+        vcopy, scopy = nc.vector.tensor_copy, nc.scalar.copy
+        interleave(0, 0, 0, 256, vcopy)
+        quantize(0, 0, 256)
+        interleave(0, 256, 256, 352, scopy)
+        interleave(0, 256, 352, 512, vcopy)
+        quantize(0, 256, 512)
+        interleave(1, 0, 0, 256, scopy)
+        interleave(1, 256, 256, 512, scopy)
+        for cut in CUTS:
+            gather_words(0, cut)
+        quantize(1, 0, 512)
+        interleave(2, 0, 0, 256, scopy)
+        interleave(2, 0, 256, 512, scopy)
+        for cut in CUTS:
+            gather_words(1, cut)
+        quantize(2, 0, 512)
+        for cut in CUTS:
+            gather_scales(cut)
+        for cut in CUTS:
+            gather_words(2, cut)
+
+        acc = {}
+        for e in range(E):
+            for c in range(BLOCKS):
+                acc[c, e] = psum.tile([P, C], F32, name="acc%d%d" % (c, e))
+        for a in range(PASSES):
+            for e in range(E):
+                cols = slice(e * C, (e + 1) * C)
+                for c in range(BLOCKS):
+                    feat = slice(c * P, (c + 1) * P)
+                    s0 = (e * PASSES + a) * N + c * P
+                    nc.tensor.matmul_mx(
+                        out=acc[c, e][:],
+                        lhsT=w_t[e][:, a, feat].bitcast(FP8X4),
+                        lhsT_scale=w_scale_t[:, s0 : s0 + P],
+                        rhs=slot_words[a][:, cols].bitcast(FP8X4),
+                        rhs_scale=slot_scales[4 * a : P, cols],
+                        start=(a == 0),
+                        stop=(a == PASSES - 1),
+                    )
+
+        y = [keep.tile([P, SLOTS], F32, name="y%d" % c) for c in range(BLOCKS)]
+        for e in range(E):
+            for c in range(BLOCKS):
+                nc.scalar.activation(y[c][:, e * C : (e + 1) * C], acc[c, e][:], SILU, bias=bias_t[:, c, e : e + 1])
+
+        term = {}
+
+        def gather_term(c, r):
+            term[c, r] = keep.tile([P, T], F32, name="term%d%d" % (c, r))
+            nc.vector.tensor_tensor(term[c, r][:], y[c][:].indirect(pos_t[r][:]), gate_t[c, r][:], MULT)
+
+        def add_and_store(c, lo, hi, queue):
+            total = keep.tile([P, hi - lo], F32, name="total%d_%d" % (c, lo))
+            nc.vector.tensor_tensor(total[:], term[c, 0][:, lo:hi], term[c, 1][:, lo:hi], ADD)
+            queue.dma_start(out=out[c * P : (c + 1) * P, lo:hi], in_=total[:])
+
+        gather_term(0, 0)
+        gather_term(0, 1)
+        gather_term(1, 0)
+        add_and_store(0, 0, T, nc.sync)
+        gather_term(1, 1)
+        add_and_store(1, 0, HALF, nc.sync)
+        add_and_store(1, HALF, T, nc.scalar)

@@ -22,8 +22,8 @@ SILU = mybir.ActivationFunctionType.Silu
 MULT = mybir.AluOpType.mult
 ADD = mybir.AluOpType.add
 
-LOADS = (((0, 256), (256, 512)), ((0, 256), (256, 512)), ((0, 512),))
-CUTS = ((0, 384), (384, 768), (768, 1024))
+LOADS = (((0, 256), (256, 512)), ((0, 256), (256, 512)), ((0, 256), (256, 512)))
+WINDOW = 3 * T
 
 
 def tile_routed_moe_kernel(tc, xT, w_words, w_scales, b, gate, offs, pos1, pos2, out):
@@ -41,7 +41,7 @@ def tile_routed_moe_kernel(tc, xT, w_words, w_scales, b, gate, offs, pos1, pos2,
         warm_out = keep.tile([P, 1], F32, name="warm_out")
         nc.scalar.activation(warm_out[:], warm[:], SILU)
 
-        token_scales = keep.tile([P, T], U8, name="token_scales", align_bytes=64)
+        token_scales = keep.tile([P, WINDOW], U8, name="token_scales", align_bytes=64)
         nc.gpsimd.memset(token_scales[:], 0)
         w_scale_t = keep.tile([P, E * PASSES * N], U8, name="w_scale_t", align_bytes=64)
         nc.vector.memset(w_scale_t[:].bitcast(I32), 0)
@@ -52,16 +52,10 @@ def tile_routed_moe_kernel(tc, xT, w_words, w_scales, b, gate, offs, pos1, pos2,
             for lo, hi in LOADS[a]:
                 raw[a, lo] = keep.tile([P, PACK, hi - lo], F32, name="raw%d_%d" % (a, lo))
                 nc.sync.dma_start(out=raw[a, lo][:], in_=rows[:, :, lo:hi])
-                if a == 0 and lo == 0:
+                if a == 0 and hi == T:
                     nc.sync.dma_start(offs_t[:], offs)
         bias_t = keep.tile([P, BLOCKS, E], F32, name="bias_t")
-        nc.scalar.dma_start(out=bias_t[:], in_=b.rearrange("(c p) e -> p c e", p=P))
         sview = w_scales.rearrange("e a q n -> q (e a) n")
-        for q in range(4):
-            nc.sync.dma_start(
-                out=w_scale_t[32 * q : 32 * q + 4, :].rearrange("p (g n) -> p g n", n=N).bitcast(I32),
-                in_=sview[4 * q : 4 * q + 4].bitcast(I32),
-            )
         w_t = {}
         for e in range(E):
             w_t[e] = keep.tile([P, PASSES, N], U32, name="w%d" % e, align_bytes=64)
@@ -69,6 +63,13 @@ def tile_routed_moe_kernel(tc, xT, w_words, w_scales, b, gate, offs, pos1, pos2,
                 out=w_t[e][:].bitcast(I32),
                 in_=w_words[e].rearrange("a p n r -> p a (n r)").bitcast(I32),
             )
+            if e == 1:
+                for q in range(4):
+                    nc.sync.dma_start(
+                        out=w_scale_t[32 * q : 32 * q + 4, :].rearrange("p (g n) -> p g n", n=N).bitcast(I32),
+                        in_=sview[4 * q : 4 * q + 4].bitcast(I32),
+                    )
+                nc.sync.dma_start(out=bias_t[:], in_=b.rearrange("(c p) e -> p c e", p=P))
         nc.sync.dma_start(pos_t[0][:], pos1)
         nc.sync.dma_start(pos_t[1][:], pos2)
         gate_t = {}
@@ -78,7 +79,9 @@ def tile_routed_moe_kernel(tc, xT, w_words, w_scales, b, gate, offs, pos1, pos2,
                 nc.sync.dma_start(out=gate_t[c, r][:], in_=gate[r, c * P : (c + 1) * P, :])
 
         grouped = [keep.tile([P, T, PACK], BF16, name="grouped%d" % a, align_bytes=64) for a in range(PASSES)]
-        token_words = [keep.tile([P, T], U32, name="token_words%d" % a, align_bytes=64) for a in range(PASSES)]
+        token_words = keep.tile([P, (PASSES - 1) * T + WINDOW], U32, name="token_words", align_bytes=64)
+        nc.gpsimd.memset(token_words[:, PASSES * T :].bitcast(I32), 0)
+        first_col = [(PASSES - 1 - a) * T for a in range(PASSES)]
         slot_words = [keep.tile([P, SLOTS], U32, name="slot_words%d" % a, align_bytes=64) for a in range(PASSES)]
         slot_scales = keep.tile([P, SLOTS], U8, name="slot_scales", align_bytes=64)
 
@@ -87,17 +90,16 @@ def tile_routed_moe_kernel(tc, xT, w_words, w_scales, b, gate, offs, pos1, pos2,
 
         def quantize(a, lo, hi):
             nc.vector.quantize_mx(
-                out=token_words[a][:, lo:hi].bitcast(FP8X4),
+                out=token_words[:, first_col[a] + lo : first_col[a] + hi].bitcast(FP8X4),
                 scales=token_scales[4 * a : P, lo:hi],
                 in_=grouped[a][:, lo:hi, :].rearrange("p n t -> p (n t)"),
             )
 
-        def gather_words(a, cut):
-            lo, hi = cut
-            nc.vector.tensor_copy(slot_words[a][:, lo:hi], token_words[a][:].indirect(offs_t[:, lo // 16 : hi // 16]))
+        def gather_words(a, lo, hi):
+            window = token_words[:, first_col[a] : first_col[a] + WINDOW]
+            nc.vector.tensor_copy(slot_words[a][:, lo:hi], window.indirect(offs_t[:, lo // 16 : hi // 16]))
 
-        def gather_scales(cut):
-            lo, hi = cut
+        def gather_scales(lo, hi):
             nc.vector.tensor_copy(slot_scales[:, lo:hi], token_scales[:].indirect(offs_t[:, lo // 16 : hi // 16]))
 
         vcopy, scopy = nc.vector.tensor_copy, nc.scalar.copy
@@ -108,42 +110,46 @@ def tile_routed_moe_kernel(tc, xT, w_words, w_scales, b, gate, offs, pos1, pos2,
         quantize(0, 256, 512)
         interleave(1, 0, 0, 256, scopy)
         interleave(1, 256, 256, 512, scopy)
-        for cut in CUTS:
-            gather_words(0, cut)
+        gather_words(0, 0, 1024)
         quantize(1, 0, 512)
         interleave(2, 0, 0, 256, scopy)
-        interleave(2, 0, 256, 512, scopy)
-        for cut in CUTS:
-            gather_words(1, cut)
+        interleave(2, 256, 256, 512, scopy)
+        gather_words(1, 0, 512)
         quantize(2, 0, 512)
-        for cut in CUTS:
-            gather_scales(cut)
-        for cut in CUTS:
-            gather_words(2, cut)
+        gather_scales(0, 512)
+        gather_scales(512, 1024)
+        gather_words(1, 512, 1024)
+        gather_words(2, 0, 512)
+        gather_words(2, 512, 768)
+        gather_words(2, 768, 1024)
 
         acc = {}
         for e in range(E):
             for c in range(BLOCKS):
                 acc[c, e] = psum.tile([P, C], F32, name="acc%d%d" % (c, e))
-        for a in range(PASSES):
-            for e in range(E):
-                cols = slice(e * C, (e + 1) * C)
-                for c in range(BLOCKS):
-                    feat = slice(c * P, (c + 1) * P)
-                    s0 = (e * PASSES + a) * N + c * P
-                    nc.tensor.matmul_mx(
-                        out=acc[c, e][:],
-                        lhsT=w_t[e][:, a, feat].bitcast(FP8X4),
-                        lhsT_scale=w_scale_t[:, s0 : s0 + P],
-                        rhs=slot_words[a][:, cols].bitcast(FP8X4),
-                        rhs_scale=slot_scales[4 * a : P, cols],
-                        start=(a == 0),
-                        stop=(a == PASSES - 1),
-                    )
-
         y = [keep.tile([P, SLOTS], F32, name="y%d" % c) for c in range(BLOCKS)]
+
+        def multiply(e, c, a):
+            cols = slice(e * C, (e + 1) * C)
+            s0 = (e * PASSES + a) * N + c * P
+            nc.tensor.matmul_mx(
+                out=acc[c, e][:],
+                lhsT=w_t[e][:, a, c * P : (c + 1) * P].bitcast(FP8X4),
+                lhsT_scale=w_scale_t[:, s0 : s0 + P],
+                rhs=slot_words[a][:, cols].bitcast(FP8X4),
+                rhs_scale=slot_scales[4 * a : P, cols],
+                start=(a == 0),
+                stop=(a == PASSES - 1),
+            )
+
+        for pair in ((0, 1), (2, 3)):
+            for a in range(2):
+                for e in pair:
+                    for c in range(BLOCKS):
+                        multiply(e, c, a)
         for e in range(E):
             for c in range(BLOCKS):
+                multiply(e, c, 2)
                 nc.scalar.activation(y[c][:, e * C : (e + 1) * C], acc[c, e][:], SILU, bias=bias_t[:, c, e : e + 1])
 
         term = {}

@@ -42,7 +42,7 @@ def tile_routed_moe_kernel(tc, xT, w_words, w_scales, b, gate, offs, pos1, pos2,
         nc.scalar.activation(warm_out[:], warm[:], SILU)
 
         token_scales = keep.tile([P, WINDOW], U8, name="token_scales", align_bytes=64)
-        nc.gpsimd.memset(token_scales[:], 0)
+        nc.vector.memset(token_scales[:].bitcast(I32), 0)
         w_scale_t = keep.tile([P, E * PASSES * N], U8, name="w_scale_t", align_bytes=64)
         nc.vector.memset(w_scale_t[:].bitcast(I32), 0)
 
@@ -80,13 +80,16 @@ def tile_routed_moe_kernel(tc, xT, w_words, w_scales, b, gate, offs, pos1, pos2,
 
         grouped = [keep.tile([P, T, PACK], BF16, name="grouped%d" % a, align_bytes=64) for a in range(PASSES)]
         token_words = keep.tile([P, (PASSES - 1) * T + WINDOW], U32, name="token_words", align_bytes=64)
-        nc.gpsimd.memset(token_words[:, PASSES * T :].bitcast(I32), 0)
+        nc.vector.memset(token_words[:, PASSES * T :].bitcast(I32), 0)
         first_col = [(PASSES - 1 - a) * T for a in range(PASSES)]
         slot_words = [keep.tile([P, SLOTS], U32, name="slot_words%d" % a, align_bytes=64) for a in range(PASSES)]
         slot_scales = keep.tile([P, SLOTS], U8, name="slot_scales", align_bytes=64)
 
         def interleave(a, load, lo, hi, copy):
-            copy(grouped[a][:, lo:hi, :], raw[a, load][:, :, lo - load : hi - load].rearrange("p t n -> p n t"))
+            copy(
+                grouped[a][:, lo:hi, :].rearrange("p (c i) t -> p c t i", i=4),
+                raw[a, load][:, :, lo - load : hi - load].rearrange("p t (c i) -> p c t i", i=4),
+            )
 
         def quantize(a, lo, hi):
             nc.vector.quantize_mx(
@@ -114,11 +117,11 @@ def tile_routed_moe_kernel(tc, xT, w_words, w_scales, b, gate, offs, pos1, pos2,
         quantize(1, 0, 512)
         interleave(2, 0, 0, 256, scopy)
         interleave(2, 256, 256, 512, scopy)
-        gather_words(1, 0, 512)
+        gather_words(1, 0, 1024)
         quantize(2, 0, 512)
-        gather_scales(0, 512)
+        gather_scales(0, 256)
+        gather_scales(256, 512)
         gather_scales(512, 1024)
-        gather_words(1, 512, 1024)
         gather_words(2, 0, 512)
         gather_words(2, 512, 768)
         gather_words(2, 768, 1024)
@@ -142,15 +145,14 @@ def tile_routed_moe_kernel(tc, xT, w_words, w_scales, b, gate, offs, pos1, pos2,
                 stop=(a == PASSES - 1),
             )
 
-        for pair in ((0, 1), (2, 3)):
-            for a in range(2):
-                for e in pair:
-                    for c in range(BLOCKS):
-                        multiply(e, c, a)
         for e in range(E):
-            for c in range(BLOCKS):
-                multiply(e, c, 2)
-                nc.scalar.activation(y[c][:, e * C : (e + 1) * C], acc[c, e][:], SILU, bias=bias_t[:, c, e : e + 1])
+            for a in range(2):
+                for c in range(BLOCKS):
+                    multiply(e, c, a)
+        for e, c in ((0, 0), (1, 0), (0, 1), (1, 1), (2, 0), (2, 1), (3, 0), (3, 1)):
+            multiply(e, c, 2)
+        for e, c in ((0, 0), (1, 0), (0, 1), (2, 0), (3, 0), (1, 1), (2, 1), (3, 1)):
+            nc.scalar.activation(y[c][:, e * C : (e + 1) * C], acc[c, e][:], SILU, bias=bias_t[:, c, e : e + 1])
 
         term = {}
 

@@ -1,6 +1,7 @@
 from contextlib import ExitStack
 
 import concourse.mybir as mybir
+from concourse.masks import make_identity
 
 K, T, E, C, N = 1536, 512, 4, 256, 256
 P = 128
@@ -45,6 +46,9 @@ def tile_routed_moe_kernel(tc, xT, w_words, w_scales, b, gate, offs, pos1, pos2,
         nc.vector.memset(token_scales[:].bitcast(I32), 0)
         w_scale_t = keep.tile([P, E * PASSES * N], U8, name="w_scale_t", align_bytes=64)
         nc.vector.memset(w_scale_t[:].bitcast(I32), 0)
+
+        ident = keep.tile([P, P], F32, name="ident")
+        make_identity(nc, ident[:])
 
         raw = {}
         for a in range(PASSES):
@@ -112,11 +116,13 @@ def tile_routed_moe_kernel(tc, xT, w_words, w_scales, b, gate, offs, pos1, pos2,
         interleave(0, 256, 352, 512, vcopy)
         quantize(0, 256, 512)
         interleave(1, 0, 0, 256, scopy)
-        interleave(1, 256, 256, 512, scopy)
+        interleave(1, 256, 256, 448, scopy)
+        interleave(1, 256, 448, 512, nc.gpsimd.tensor_copy)
         gather_words(0, 0, 1024)
         quantize(1, 0, 512)
         interleave(2, 0, 0, 256, scopy)
-        interleave(2, 256, 256, 512, scopy)
+        interleave(2, 256, 256, 448, scopy)
+        interleave(2, 256, 448, 512, nc.gpsimd.tensor_copy)
         gather_words(1, 0, 1024)
         quantize(2, 0, 512)
         gather_scales(0, 256)
@@ -160,15 +166,30 @@ def tile_routed_moe_kernel(tc, xT, w_words, w_scales, b, gate, offs, pos1, pos2,
             term[c, r] = keep.tile([P, T], F32, name="term%d%d" % (c, r))
             nc.vector.tensor_tensor(term[c, r][:], y[c][:].indirect(pos_t[r][:]), gate_t[c, r][:], MULT)
 
+        halves = [(h, h * HALF, (h + 1) * HALF) for h in range(2)]
+        both = [psum.tile([P, HALF], F32, name="both%d" % h, tag="acc0%d" % h) for h in range(2)]
+
+        def add_on_tensor(c, r):
+            for h, lo, hi in halves:
+                nc.tensor.matmul(both[h][:], ident[:], term[c, r][:, lo:hi], start=(r == 0), stop=(r == 1))
+
+        def store_sums(c):
+            for h, lo, hi in halves:
+                total = keep.tile([P, HALF], F32, name="total%d_%d" % (c, lo))
+                nc.scalar.copy(total[:], both[h][:])
+                nc.sync.dma_start(out=out[c * P : (c + 1) * P, lo:hi], in_=total[:])
+
         def add_and_store(c, lo, hi, queue):
             total = keep.tile([P, hi - lo], F32, name="total%d_%d" % (c, lo))
             nc.vector.tensor_tensor(total[:], term[c, 0][:, lo:hi], term[c, 1][:, lo:hi], ADD)
             queue.dma_start(out=out[c * P : (c + 1) * P, lo:hi], in_=total[:])
 
         gather_term(0, 0)
+        add_on_tensor(0, 0)
         gather_term(0, 1)
+        add_on_tensor(0, 1)
+        store_sums(0)
         gather_term(1, 0)
-        add_and_store(0, 0, T, nc.sync)
         gather_term(1, 1)
         add_and_store(1, 0, HALF, nc.sync)
         add_and_store(1, HALF, T, nc.scalar)

from contextlib import ExitStack

import concourse.mybir as mybir
from concourse.masks import make_identity

K, T, E, C, N = 1536, 512, 4, 256, 256
P = 128
PACK = 4
PASSES = K // (P * PACK)
BLOCKS = N // P
SLOTS = E * C
HALF = T // 2
FLOPS = 2 * SLOTS * K * N

F32 = mybir.dt.float32
BF16 = mybir.dt.bfloat16
U32 = mybir.dt.uint32
I32 = mybir.dt.int32
U16 = mybir.dt.uint16
U8 = mybir.dt.uint8
FP8X4 = mybir.dt.float8_e4m3fn_x4
SILU = mybir.ActivationFunctionType.Silu
MULT = mybir.AluOpType.mult
ADD = mybir.AluOpType.add

LOADS = (((0, 256), (256, 512)), ((0, 256), (256, 512)), ((0, 256), (256, 512)))
WINDOW = 3 * T


def tile_routed_moe_kernel(tc, xT, w_words, w_scales, b, gate, offs, pos1, pos2, out):
    nc = tc.nc
    with ExitStack() as ctx:
        lists = ctx.enter_context(tc.tile_pool(name="lists", bufs=1))
        keep = ctx.enter_context(tc.tile_pool(name="keep", bufs=1))
        psum = ctx.enter_context(tc.psum_pool(name="psum", bufs=1))

        offs_t = lists.tile([P, SLOTS // 16], U16, name="offs_t")
        pos_t = [lists.tile([P, T // 16], U16, name="pos%d_t" % r) for r in range(2)]

        warm = keep.tile([P, 1], F32, name="warm")
        nc.gpsimd.memset(warm[:], 0.0)
        warm_out = keep.tile([P, 1], F32, name="warm_out")
        nc.scalar.activation(warm_out[:], warm[:], SILU)

        token_scales = keep.tile([P, WINDOW], U8, name="token_scales", align_bytes=64)
        nc.vector.memset(token_scales[:].bitcast(I32), 0)
        w_scale_t = keep.tile([P, E * PASSES * N], U8, name="w_scale_t", align_bytes=64)
        nc.vector.memset(w_scale_t[:].bitcast(I32), 0)

        ident = keep.tile([P, P], F32, name="ident")
        make_identity(nc, ident[:])

        raw = {}
        for a in range(PASSES):
            rows = xT[a * P * PACK : (a + 1) * P * PACK, :].rearrange("(p t) n -> p t n", t=PACK)
            for lo, hi in LOADS[a]:
                raw[a, lo] = keep.tile([P, PACK, hi - lo], F32, name="raw%d_%d" % (a, lo))
                nc.sync.dma_start(out=raw[a, lo][:], in_=rows[:, :, lo:hi])
                if a == 0 and hi == T:
                    nc.sync.dma_start(offs_t[:], offs)
        bias_t = keep.tile([P, BLOCKS, E], F32, name="bias_t")
        sview = w_scales.rearrange("e a q n -> q (e a) n")
        w_t = {}
        for e in range(E):
            w_t[e] = keep.tile([P, PASSES, N], U32, name="w%d" % e, align_bytes=64)
            nc.sync.dma_start(
                out=w_t[e][:].bitcast(I32),
                in_=w_words[e].rearrange("a p n r -> p a (n r)").bitcast(I32),
            )
            if e == 1:
                for q in range(4):
                    nc.sync.dma_start(
                        out=w_scale_t[32 * q : 32 * q + 4, :].rearrange("p (g n) -> p g n", n=N).bitcast(I32),
                        in_=sview[4 * q : 4 * q + 4].bitcast(I32),
                    )
                nc.sync.dma_start(out=bias_t[:], in_=b.rearrange("(c p) e -> p c e", p=P))
        nc.sync.dma_start(pos_t[0][:], pos1)
        nc.sync.dma_start(pos_t[1][:], pos2)
        gate_t = {}
        for c in range(BLOCKS):
            for r in range(2):
                gate_t[c, r] = keep.tile([P, T], F32, name="gate%d%d" % (c, r))
                nc.sync.dma_start(out=gate_t[c, r][:], in_=gate[r, c * P : (c + 1) * P, :])

        grouped = [keep.tile([P, T, PACK], BF16, name="grouped%d" % a, align_bytes=64) for a in range(PASSES)]
        token_words = keep.tile([P, (PASSES - 1) * T + WINDOW], U32, name="token_words", align_bytes=64)
        nc.vector.memset(token_words[:, PASSES * T :].bitcast(I32), 0)
        first_col = [(PASSES - 1 - a) * T for a in range(PASSES)]
        slot_words = [keep.tile([P, SLOTS], U32, name="slot_words%d" % a, align_bytes=64) for a in range(PASSES)]
        slot_scales = keep.tile([P, SLOTS], U8, name="slot_scales", align_bytes=64)

        def interleave(a, load, lo, hi, copy):
            copy(
                grouped[a][:, lo:hi, :].rearrange("p (c i) t -> p c t i", i=4),
                raw[a, load][:, :, lo - load : hi - load].rearrange("p t (c i) -> p c t i", i=4),
            )

        def quantize(a, lo, hi):
            nc.vector.quantize_mx(
                out=token_words[:, first_col[a] + lo : first_col[a] + hi].bitcast(FP8X4),
                scales=token_scales[4 * a : P, lo:hi],
                in_=grouped[a][:, lo:hi, :].rearrange("p n t -> p (n t)"),
            )

        def gather_words(a, lo, hi):
            window = token_words[:, first_col[a] : first_col[a] + WINDOW]
            nc.vector.tensor_copy(slot_words[a][:, lo:hi], window.indirect(offs_t[:, lo // 16 : hi // 16]))

        def gather_scales(lo, hi):
            nc.vector.tensor_copy(slot_scales[:, lo:hi], token_scales[:].indirect(offs_t[:, lo // 16 : hi // 16]))

        vcopy, scopy = nc.vector.tensor_copy, nc.scalar.copy
        interleave(0, 0, 0, 256, vcopy)
        quantize(0, 0, 256)
        interleave(0, 256, 256, 352, scopy)
        interleave(0, 256, 352, 512, vcopy)
        quantize(0, 256, 512)
        interleave(1, 0, 0, 256, scopy)
        interleave(1, 256, 256, 448, scopy)
        interleave(1, 256, 448, 512, nc.gpsimd.tensor_copy)
        gather_words(0, 0, 1024)
        quantize(1, 0, 512)
        interleave(2, 0, 0, 256, scopy)
        interleave(2, 256, 256, 448, scopy)
        interleave(2, 256, 448, 512, nc.gpsimd.tensor_copy)
        gather_words(1, 0, 1024)
        quantize(2, 0, 512)
        gather_scales(0, 256)
        gather_scales(256, 512)
        gather_scales(512, 1024)
        gather_words(2, 0, 512)
        gather_words(2, 512, 768)
        gather_words(2, 768, 1024)

        acc = {}
        for e in range(E):
            for c in range(BLOCKS):
                acc[c, e] = psum.tile([P, C], F32, name="acc%d%d" % (c, e))
        y = [keep.tile([P, SLOTS], F32, name="y%d" % c) for c in range(BLOCKS)]

        def multiply(e, c, a):
            cols = slice(e * C, (e + 1) * C)
            s0 = (e * PASSES + a) * N + c * P
            nc.tensor.matmul_mx(
                out=acc[c, e][:],
                lhsT=w_t[e][:, a, c * P : (c + 1) * P].bitcast(FP8X4),
                lhsT_scale=w_scale_t[:, s0 : s0 + P],
                rhs=slot_words[a][:, cols].bitcast(FP8X4),
                rhs_scale=slot_scales[4 * a : P, cols],
                start=(a == 0),
                stop=(a == PASSES - 1),
            )

        for e in range(E):
            for a in range(2):
                for c in range(BLOCKS):
                    multiply(e, c, a)
        for e, c in ((0, 0), (1, 0), (0, 1), (1, 1), (2, 0), (2, 1), (3, 0), (3, 1)):
            multiply(e, c, 2)
        for e, c in ((0, 0), (1, 0), (0, 1), (2, 0), (3, 0), (1, 1), (2, 1), (3, 1)):
            nc.scalar.activation(y[c][:, e * C : (e + 1) * C], acc[c, e][:], SILU, bias=bias_t[:, c, e : e + 1])

        term = {}

        def gather_term(c, r):
            term[c, r] = keep.tile([P, T], F32, name="term%d%d" % (c, r))
            nc.vector.tensor_tensor(term[c, r][:], y[c][:].indirect(pos_t[r][:]), gate_t[c, r][:], MULT)

        halves = [(h, h * HALF, (h + 1) * HALF) for h in range(2)]
        both = [psum.tile([P, HALF], F32, name="both%d" % h, tag="acc0%d" % h) for h in range(2)]

        def add_on_tensor(c, r):
            for h, lo, hi in halves:
                nc.tensor.matmul(both[h][:], ident[:], term[c, r][:, lo:hi], start=(r == 0), stop=(r == 1))

        def store_sums(c):
            for h, lo, hi in halves:
                total = keep.tile([P, HALF], F32, name="total%d_%d" % (c, lo))
                nc.scalar.copy(total[:], both[h][:])
                nc.sync.dma_start(out=out[c * P : (c + 1) * P, lo:hi], in_=total[:])

        def add_and_store(c, lo, hi, queue):
            total = keep.tile([P, hi - lo], F32, name="total%d_%d" % (c, lo))
            nc.vector.tensor_tensor(total[:], term[c, 0][:, lo:hi], term[c, 1][:, lo:hi], ADD)
            queue.dma_start(out=out[c * P : (c + 1) * P, lo:hi], in_=total[:])

        gather_term(0, 0)
        add_on_tensor(0, 0)
        gather_term(0, 1)
        add_on_tensor(0, 1)
        store_sums(0)
        gather_term(1, 0)
        gather_term(1, 1)
        add_and_store(1, 0, HALF, nc.sync)
        add_and_store(1, HALF, T, nc.scalar)
